import numpy as np
import ml_dtypes


def mxq(x, axis, fmt="e4m3"):
    dtype, down = {"e4m3": (ml_dtypes.float8_e4m3fn, 7), "e5m2": (ml_dtypes.float8_e5m2, 14)}[fmt]
    v = np.moveaxis(np.asarray(x, np.float32).astype(ml_dtypes.bfloat16).astype(np.float64), axis, -1)
    blocks = v.reshape(v.shape[:-1] + (-1, 32))
    amax = np.abs(blocks).max(-1, keepdims=True)
    byte = np.maximum(np.where(amax > 0, np.frexp(amax)[1] - 1 + 127, 0) - down, 1)
    scale = np.exp2(byte - 127.0)
    codes = (blocks / scale).astype(np.float32).astype(dtype).astype(np.float64)
    return np.moveaxis((codes * scale).reshape(v.shape), -1, axis)


WIDE = False


def mx_kscale(k):
    if not WIDE:
        return np.ones(k)
    levels = np.array([10, -10, 5, -5, 0])
    if k % 512:
        return np.exp2(np.random.permutation(np.resize(levels, k // 32))).repeat(32)
    a = np.empty((k // 512, 16))
    for p in range(k // 512):
        a[p, :8] = np.random.permutation(np.resize(levels, 8))
        for g in range(8):
            far = levels[np.abs(levels - a[p, g]) >= 10]
            a[p, g + 8] = far[np.random.randint(len(far))]
    return np.exp2(a.ravel()).repeat(32)


def f64(x):
    return np.asarray(x).astype(np.float64)


def striped(idx):
    return np.tile(np.asarray(idx).reshape(-1, 16).T, (8, 1)).astype(np.uint16)


def unstriped(offs):
    return offs[:16].T.reshape(-1).astype(np.int64)


E2M1 = np.array([0.0, 0.5, 1.0, 1.5, 2.0, 3.0, 4.0, 6.0, -0.0, -0.5, -1.0, -1.5, -2.0, -3.0, -4.0, -6.0])


def pack_weight(w, fmt):
    k, n = w.shape
    w = f64(np.asarray(w, np.float32).astype(ml_dtypes.bfloat16)).reshape(k // 32, 32, n)
    amax = np.abs(w).max(1)
    if fmt == "e4m3":
        byte = np.frexp(amax)[1] - 1 + 127 - 7
    else:
        mant, ex = np.frexp(amax / 6.0)
        byte = np.where(mant > 0.5, ex, ex - 1) + 127
    byte = np.clip(np.where(amax > 0, byte, 1), 1, 254)
    scaled = (w * np.exp2(127.0 - byte)[:, None, :]).reshape(k, n).astype(np.float32)
    by_word = np.ascontiguousarray(scaled.reshape(k // 512, 128, 4, n).transpose(0, 1, 3, 2))
    if fmt == "e4m3":
        words = by_word.astype(ml_dtypes.float8_e4m3fn).view(np.uint8)
    else:
        c = by_word.astype(ml_dtypes.float4_e2m1fn).view(np.uint8) & 0xF
        words = (c[..., 0::2] | (c[..., 1::2] << 4)).reshape(k // 512, 128, 2 * n)
    return np.ascontiguousarray(words), np.ascontiguousarray(byte.astype(np.uint8).reshape(k // 512, 16, n))


def unpack_weight(words, scales, fmt):
    g, _, n = scales.shape
    words = np.ascontiguousarray(words).reshape(g, 128, n, -1)
    if fmt == "e4m3":
        vals = words.view(ml_dtypes.float8_e4m3fn).astype(np.float64)
    else:
        nib = np.empty((g, 128, n, 4), np.uint8)
        nib[..., 0::2] = words & 0xF
        nib[..., 1::2] = words >> 4
        vals = E2M1[nib]
    vals = vals * np.repeat(np.exp2(scales.astype(np.float64) - 127.0), 8, axis=1)[..., None]
    return vals.transpose(0, 1, 3, 2).reshape(g * 512, n)


B, N, T, D, DV, NQ = 1, 1024, 2048, 1024, 128, 256


def setup_inputs():
    n = np.random.standard_normal
    idx = np.random.permutation(T)[:B * N]
    s = mx_kscale(D)[:, None]
    u = np.ones(T)
    u[idx] = mx_kscale(B * N)
    r = np.random.uniform(0.5, 2.0, T)
    qp = [pack_weight(x, "e4m3") for x in n((B, D, NQ)) * s * (1.00 / np.sqrt(D))]
    k = n((D, T)) / s
    v = n((DV, T)) / (u * r)
    kp = pack_weight(k, "e2m1")
    return {
        "q_words": np.stack([x[0] for x in qp]),
        "q_scales": np.stack([x[1] for x in qp]),
        "k_words": np.ascontiguousarray(kp[0].reshape(D // 1024, 2, 128, T, 2).transpose(0, 2, 3, 1, 4)).reshape(D // 1024, 128, T, 4),
        "k_scales": kp[1],
        "vT": v.astype(np.float32),
        "vs": np.tile(u * r, (128, 1)).astype(np.float32),
        "og": n((B, NQ, DV)).astype(np.float32),
        "offs": striped(idx),
    }


def reference(q_words, q_scales, k_words, k_scales, vT, vs, og, offs):
    idx = unstriped(offs)
    k = unpack_weight(k_words.reshape(D // 1024, 128, T, 2, 2).transpose(0, 3, 1, 2, 4).reshape(D // 512, 128, 2 * T), k_scales, "e2m1")
    v = f64(vT)
    pick = lambda x: x[:, idx].reshape(x.shape[0], B, N).transpose(1, 0, 2)
    q = np.stack([unpack_weight(q_words[b], q_scales[b], "e4m3") for b in range(B)])
    score = q.transpose(0, 2, 1) @ pick(k)
    p = score / (1.0 + np.exp(-score))
    w = p * pick(f64(vs))[:, :1, :]
    y = mxq(w, 2, "e4m3") @ mxq(pick(v).transpose(0, 2, 1), 1, "e4m3")
    y = y / 16.0
    y = y / (1.0 + np.exp(-f64(og)))
    return y

@@ -1,0 +1,182 @@
+from contextlib import ExitStack
+
+import concourse.mybir as mybir
+from concourse.masks import make_identity
+
+F32 = mybir.dt.float32
+BF16 = mybir.dt.bfloat16
+I32 = mybir.dt.int32
+U32 = mybir.dt.uint32
+U16 = mybir.dt.uint16
+U8 = mybir.dt.uint8
+FP8X4 = mybir.dt.float8_e4m3fn_x4
+FP4X4 = mybir.dt.float4_e2m1fn_x4
+ACT = mybir.ActivationFunctionType
+MULT = mybir.AluOpType.mult
+
+P = 128
+PACK = 4
+SLOTS = 1024
+POOL = 2048
+D = 1024
+DV = 128
+NQ = 256
+PASS = P * PACK
+D_PASSES = D // PASS
+S_PASSES = SLOTS // PASS
+Q_BLOCKS = NQ // P
+QUAD = 32
+LIST_COLS = PASS // 16
+KS_ROW = P - QUAD
+VS_ROW = P - 1
+
+FLOPS = 2 * NQ * SLOTS * D + 2 * NQ * SLOTS * DV
+
+
+def tile_attend_silu_gate_topkq256n1024t2048_kernel(tc, q_words, q_scales, k_words, k_scales, vT, vs, og, offs, out):
+    nc = tc.nc
+    with ExitStack() as ctx:
+        sb = ctx.enter_context(tc.tile_pool(name="sb", bufs=1))
+        ps = ctx.enter_context(tc.psum_pool(name="ps", bufs=1))
+
+        def tile(name, shape, dtype):
+            return sb.tile(shape, dtype, name=name, align_bytes=64)
+
+        offsets = sb.tile([P, SLOTS // 16], U16, name="offsets")
+        ks_pool = tile("ks_pool", [P, POOL], U8)
+        kw_pool = tile("kw_pool", [P, POOL], U32)
+        vs_pool = tile("vs_pool", [P, POOL], F32)
+        v_raw = [tile(f"v_raw{h}", [P, POOL // 2], F32) for h in range(2)]
+        v_pool = tile("v_pool", [P, POOL], BF16)
+        qw = tile("qw", [P, D_PASSES, NQ], U32)
+        qs = tile("qs", [P, D_PASSES, NQ], U8)
+        og_sb = tile("og_sb", [P, Q_BLOCKS, DV], F32)
+        ks_plane = tile("ks_plane", [P, D_PASSES * SLOTS], U8)
+        zero = tile("zero", [P, 1], F32)
+        zero_bias = tile("zero_bias", [P, 1], F32)
+        ident = tile("ident", [P, P], F32)
+
+        nc.vector.memset(zero[:], 0.0)
+        nc.vector.memset(qs[:].rearrange("p o q -> p (o q)").bitcast(I32), 0)
+        nc.vector.memset(ks_pool[:KS_ROW, :].bitcast(I32), 0)
+        nc.vector.memset(vs_pool[:VS_ROW, :], 0.0)
+        nc.vector.memset(ks_plane[:].bitcast(I32), 0)
+        nc.scalar.activation(zero_bias[:], zero[:], ACT.Silu)
+        make_identity(nc, ident[:])
+
+        nc.sync.dma_start(offsets[:], offs)
+        nc.sync.dma_start(ks_pool[KS_ROW:, :].bitcast(I32), k_scales.rearrange("o f t -> (o f) t").bitcast(I32))
+        nc.sync.dma_start(vs_pool[VS_ROW:, :], vs[0:1, :])
+        for h in range(2):
+            nc.sync.dma_start(v_raw[h][:], vT[:, h * POOL // 2 : (h + 1) * POOL // 2])
+        nc.sync.dma_start(kw_pool[:].bitcast(I32), k_words[0].rearrange("p t b -> p (t b)").bitcast(I32))
+        nc.sync.dma_start(qw[:].bitcast(I32), q_words[0].rearrange("o p q r -> p o (q r)").bitcast(I32))
+        for quad in range(4):
+            nc.sync.dma_start(
+                qs[QUAD * quad : QUAD * quad + 4, :, :].bitcast(I32),
+                q_scales[0, :, 4 * quad : 4 * quad + 4, :].rearrange("o f q -> f o q").bitcast(I32),
+            )
+        nc.sync.dma_start(og_sb[:], og[0].rearrange("(b p) e -> p b e", p=P))
+
+        ks_got = tile("ks_got", [P, SLOTS], U8)
+        nc.vector.tensor_copy(ks_got[:], ks_pool[:].indirect(offsets[:]))
+        ks_dealt = tile("ks_dealt", [P, SLOTS], U8)
+        nc.vector.tensor_copy(
+            ks_dealt[:].rearrange("p (g r b s) -> p g b r s", g=S_PASSES, r=PACK, s=16),
+            ks_got[:].rearrange("p (g b s r) -> p g b r s", g=S_PASSES, r=PACK, s=16),
+        )
+        for o in range(D_PASSES):
+            for quad in range(4):
+                row = KS_ROW + 16 * o + 4 * quad
+                nc.sync.dma_start(
+                    ks_plane[QUAD * quad : QUAD * quad + 4, o * SLOTS : (o + 1) * SLOTS].bitcast(I32),
+                    ks_dealt[row : row + 4, :].bitcast(I32),
+                )
+
+        vs_cols = ps.tile([P, PASS], F32, name="vs_cols")
+        for g in range(S_PASSES):
+            vs_got = tile(f"vs_got{g}", [P, PASS], F32)
+            nc.vector.tensor_copy(vs_got[:], vs_pool[:].indirect(offsets[:, g * LIST_COLS : (g + 1) * LIST_COLS]))
+            for r in reversed(range(PACK)):
+                c = 2 * (PACK * (S_PASSES - 1 - g) + r)
+                nc.tensor.transpose(vs_cols[:, c : c + P], vs_got[:, r:PASS:PACK], ident[:])
+
+        for h in range(2):
+            nc.scalar.activation(v_pool[:, h * POOL // 2 : (h + 1) * POOL // 2], v_raw[h][:], ACT.Copy)
+        v_got = tile("v_got", [P, SLOTS], BF16)
+        nc.scalar.activation(v_got[:], v_pool[:].indirect(offsets[:]), ACT.Copy)
+        v_pairs = v_got[:].bitcast(F32)
+        v_turned = ps.tile([P, S_PASSES, 2, DV], F32, name="v_turned")
+        for g in range(S_PASSES):
+            for u in range(2):
+                nc.tensor.transpose(v_turned[:, g, u, :], v_pairs[:, 256 * g + u : 256 * (g + 1) : 2], ident[:])
+        v_woven = tile("v_woven", [P, S_PASSES * DV * PACK], BF16)
+        nc.scalar.copy(
+            v_woven[:].bitcast(F32).rearrange("p (g e u) -> p g e u", g=S_PASSES, u=2),
+            v_turned[:].rearrange("p g u e -> p g e u"),
+        )
+
+        th = tile("th", [P, Q_BLOCKS, DV], F32)
+        gate = tile("gate", [P, Q_BLOCKS, DV], F32)
+        nc.scalar.activation(th[:], og_sb[:], ACT.Tanh, bias=zero_bias[:], scale=0.5)
+        nc.scalar.activation(gate[:], th[:], ACT.Copy, bias=1.0 / 32.0, scale=1.0 / 32.0)
+
+        p_woven = {}
+        for g in range(S_PASSES):
+            kw_got = tile("kw_got", [P, PASS], U32)
+            nc.vector.tensor_copy(kw_got[:], kw_pool[:].indirect(offsets[:, g * LIST_COLS : (g + 1) * LIST_COLS]))
+            kw = tile(f"kw{g}", [P, D_PASSES, PASS], U16)
+            nc.vector.tensor_copy(
+                kw[:].rearrange("p o (r b s) -> p o b r s", r=PACK, s=4),
+                kw_got[:].bitcast(U16).rearrange("p (b s r o) -> p o b r s", o=D_PASSES, r=PACK, s=4),
+            )
+            for b in range(Q_BLOCKS):
+                scores = ps.tile([P, PACK, P], F32, name=f"scores{g}{b}")
+                for r in range(PACK):
+                    for o in range(D_PASSES):
+                        nc.tensor.matmul_mx(
+                            out=scores[:, r, :],
+                            lhsT=kw[:, o, r * P : (r + 1) * P].bitcast(FP4X4),
+                            lhsT_scale=ks_plane[:, o * SLOTS + g * PASS + r * P : o * SLOTS + g * PASS + (r + 1) * P],
+                            rhs=qw[:, o, b * P : (b + 1) * P].bitcast(FP8X4),
+                            rhs_scale=qs[:, o, b * P : (b + 1) * P],
+                            start=(o == 0),
+                            stop=(o == D_PASSES - 1),
+                        )
+                p_woven[g, b] = tile(f"p{g}{b}", [P, P, PACK], F32)
+                nc.scalar.activation(p_woven[g, b][:], scores[:].rearrange("p r q -> p q r"), ACT.Silu, bias=zero_bias[:])
+
+        v_codes = tile("v_codes", [P, S_PASSES * DV], U32)
+        v_scales = tile("v_scales", [P, S_PASSES * DV], U8)
+        nc.vector.quantize_mx(out=v_codes[:].bitcast(FP8X4), scales=v_scales[:], in_=v_woven[:])
+
+        w_codes, w_scales = {}, {}
+        for g in range(S_PASSES):
+            first = 2 * PACK * (S_PASSES - 1 - g) + VS_ROW
+            vs_by_place = vs_cols[:, first : first + 2 * PACK : 2].unsqueeze(1).to_broadcast([P, P, PACK])
+            for b in range(Q_BLOCKS):
+                w = tile(f"w{g}{b}", [P, P, PACK], BF16)
+                nc.vector.tensor_tensor(w[:], p_woven[g, b][:], vs_by_place, MULT)
+                w_codes[g, b] = tile(f"w_codes{g}{b}", [P, P], U32)
+                w_scales[g, b] = tile(f"w_scales{g}{b}", [P, P], U8)
+                nc.vector.quantize_mx(
+                    out=w_codes[g, b][:].bitcast(FP8X4),
+                    scales=w_scales[g, b][:],
+                    in_=w[:].rearrange("p q r -> p (q r)"),
+                )
+
+        for b in range(Q_BLOCKS):
+            y = ps.tile([P, DV], F32, name=f"y{b}")
+            for g in range(S_PASSES):
+                nc.tensor.matmul_mx(
+                    out=y[:],
+                    lhsT=w_codes[g, b][:].bitcast(FP8X4),
+                    lhsT_scale=w_scales[g, b][:],
+                    rhs=v_codes[:, g * DV : (g + 1) * DV].bitcast(FP8X4),
+                    rhs_scale=v_scales[:, g * DV : (g + 1) * DV],
+                    start=(g == 0),
+                    stop=(g == S_PASSES - 1),
+                )
+            res = tile(f"res{b}", [P, DV], F32)
+            nc.vector.tensor_tensor(res[:], y[:], gate[:, b, :], MULT)
+            nc.sync.dma_start(out[0, b * P : (b + 1) * P, :], res[:])

@@ -27,6 +27,7 @@ S_PASSES = SLOTS // PASS
 Q_BLOCKS = NQ // P
 QUAD = 32
 LIST_COLS = PASS // 16
+V_PIECE = 512
 KS_ROW = P - QUAD
 VS_ROW = P - 1
 
@@ -46,7 +47,7 @@ def tile_attend_silu_gate_topkq256n1024t2048_kernel(tc, q_words, q_scales, k_wor
         ks_pool = tile("ks_pool", [P, POOL], U8)
         kw_pool = tile("kw_pool", [P, POOL], U32)
         vs_pool = tile("vs_pool", [P, POOL], F32)
-        v_raw = [tile(f"v_raw{h}", [P, POOL // 2], F32) for h in range(2)]
+        v_raw = [tile(f"v_raw{h}", [P, V_PIECE], F32) for h in range(POOL // V_PIECE)]
         v_pool = tile("v_pool", [P, POOL], BF16)
         qw = tile("qw", [P, D_PASSES, NQ], U32)
         qs = tile("qs", [P, D_PASSES, NQ], U8)
@@ -57,18 +58,19 @@ def tile_attend_silu_gate_topkq256n1024t2048_kernel(tc, q_words, q_scales, k_wor
         ident = tile("ident", [P, P], F32)
 
         nc.vector.memset(zero[:], 0.0)
-        nc.vector.memset(qs[:].rearrange("p o q -> p (o q)").bitcast(I32), 0)
-        nc.vector.memset(ks_pool[:KS_ROW, :].bitcast(I32), 0)
-        nc.vector.memset(vs_pool[:VS_ROW, :], 0.0)
-        nc.vector.memset(ks_plane[:].bitcast(I32), 0)
+        nc.gpsimd.memset(ks_pool[:KS_ROW, :].bitcast(I32), 0)
+        nc.gpsimd.memset(qs[:].rearrange("p o q -> p (o q)").bitcast(I32), 0)
+        nc.gpsimd.memset(vs_pool[:VS_ROW, :], 0.0)
+        nc.gpsimd.memset(ks_plane[:].bitcast(I32), 0)
         nc.scalar.activation(zero_bias[:], zero[:], ACT.Silu)
         make_identity(nc, ident[:])
 
         nc.sync.dma_start(offsets[:], offs)
         nc.sync.dma_start(ks_pool[KS_ROW:, :].bitcast(I32), k_scales.rearrange("o f t -> (o f) t").bitcast(I32))
         nc.sync.dma_start(vs_pool[VS_ROW:, :], vs[0:1, :])
-        for h in range(2):
-            nc.sync.dma_start(v_raw[h][:], vT[:, h * POOL // 2 : (h + 1) * POOL // 2])
+        nc.sync.dma_start(og_sb[:], og[0].rearrange("(b p) e -> p b e", p=P))
+        for h, piece in enumerate(v_raw):
+            nc.sync.dma_start(piece[:], vT[:, h * V_PIECE : (h + 1) * V_PIECE])
         nc.sync.dma_start(kw_pool[:].bitcast(I32), k_words[0].rearrange("p t b -> p (t b)").bitcast(I32))
         nc.sync.dma_start(qw[:].bitcast(I32), q_words[0].rearrange("o p q r -> p o (q r)").bitcast(I32))
         for quad in range(4):
@@ -76,7 +78,6 @@ def tile_attend_silu_gate_topkq256n1024t2048_kernel(tc, q_words, q_scales, k_wor
                 qs[QUAD * quad : QUAD * quad + 4, :, :].bitcast(I32),
                 q_scales[0, :, 4 * quad : 4 * quad + 4, :].rearrange("o f q -> f o q").bitcast(I32),
             )
-        nc.sync.dma_start(og_sb[:], og[0].rearrange("(b p) e -> p b e", p=P))
 
         ks_got = tile("ks_got", [P, SLOTS], U8)
         nc.vector.tensor_copy(ks_got[:], ks_pool[:].indirect(offsets[:]))
@@ -85,7 +86,7 @@ def tile_attend_silu_gate_topkq256n1024t2048_kernel(tc, q_words, q_scales, k_wor
             ks_dealt[:].rearrange("p (g r b s) -> p g b r s", g=S_PASSES, r=PACK, s=16),
             ks_got[:].rearrange("p (g b s r) -> p g b r s", g=S_PASSES, r=PACK, s=16),
         )
-        for o in range(D_PASSES):
+        for o in reversed(range(D_PASSES)):
             for quad in range(4):
                 row = KS_ROW + 16 * o + 4 * quad
                 nc.sync.dma_start(
@@ -101,15 +102,15 @@ def tile_attend_silu_gate_topkq256n1024t2048_kernel(tc, q_words, q_scales, k_wor
                 c = 2 * (PACK * (S_PASSES - 1 - g) + r)
                 nc.tensor.transpose(vs_cols[:, c : c + P], vs_got[:, r:PASS:PACK], ident[:])
 
-        for h in range(2):
-            nc.scalar.activation(v_pool[:, h * POOL // 2 : (h + 1) * POOL // 2], v_raw[h][:], ACT.Copy)
-        v_got = tile("v_got", [P, SLOTS], BF16)
-        nc.scalar.activation(v_got[:], v_pool[:].indirect(offsets[:]), ACT.Copy)
-        v_pairs = v_got[:].bitcast(F32)
+        for h, piece in enumerate(v_raw):
+            nc.scalar.activation(v_pool[:, h * V_PIECE : (h + 1) * V_PIECE], piece[:], ACT.Copy)
         v_turned = ps.tile([P, S_PASSES, 2, DV], F32, name="v_turned")
         for g in range(S_PASSES):
+            v_got = tile(f"v_got{g}", [P, PASS], BF16)
+            nc.scalar.activation(v_got[:], v_pool[:].indirect(offsets[:, g * LIST_COLS : (g + 1) * LIST_COLS]), ACT.Copy)
+            v_pairs = v_got[:].bitcast(F32)
             for u in range(2):
-                nc.tensor.transpose(v_turned[:, g, u, :], v_pairs[:, 256 * g + u : 256 * (g + 1) : 2], ident[:])
+                nc.tensor.transpose(v_turned[:, g, u, :], v_pairs[:, u : PASS // 2 : 2], ident[:])
         v_woven = tile("v_woven", [P, S_PASSES * DV * PACK], BF16)
         nc.scalar.copy(
             v_woven[:].bitcast(F32).rearrange("p (g e u) -> p g e u", g=S_PASSES, u=2),

@@ -64,6 +64,8 @@ def tile_attend_silu_gate_topkq256n1024t2048_kernel(tc, q_words, q_scales, k_wor
         nc.gpsimd.memset(ks_plane[:].bitcast(I32), 0)
         nc.scalar.activation(zero_bias[:], zero[:], ACT.Silu)
         make_identity(nc, ident[:])
+        ident16 = tile("ident16", [P, P], BF16)
+        make_identity(nc, ident16[:])
 
         nc.sync.dma_start(offsets[:], offs)
         nc.sync.dma_start(ks_pool[KS_ROW:, :].bitcast(I32), k_scales.rearrange("o f t -> (o f) t").bitcast(I32))
@@ -83,8 +85,8 @@ def tile_attend_silu_gate_topkq256n1024t2048_kernel(tc, q_words, q_scales, k_wor
         nc.vector.tensor_copy(ks_got[:], ks_pool[:].indirect(offsets[:]))
         ks_dealt = tile("ks_dealt", [P, SLOTS], U8)
         nc.vector.tensor_copy(
-            ks_dealt[:].rearrange("p (g r b s) -> p g b r s", g=S_PASSES, r=PACK, s=16),
-            ks_got[:].rearrange("p (g b s r) -> p g b r s", g=S_PASSES, r=PACK, s=16),
+            ks_dealt[:].bitcast(I32).rearrange("p (g r b w) -> p g b r w", g=S_PASSES, r=PACK, w=2),
+            ks_got[:].bitcast(I32).rearrange("p (g b r w) -> p g b r w", g=S_PASSES, r=PACK, w=2),
         )
         for o in reversed(range(D_PASSES)):
             for quad in range(4):
@@ -97,24 +99,30 @@ def tile_attend_silu_gate_topkq256n1024t2048_kernel(tc, q_words, q_scales, k_wor
         vs_cols = ps.tile([P, PASS], F32, name="vs_cols")
         for g in range(S_PASSES):
             vs_got = tile(f"vs_got{g}", [P, PASS], F32)
-            nc.vector.tensor_copy(vs_got[:], vs_pool[:].indirect(offsets[:, g * LIST_COLS : (g + 1) * LIST_COLS]))
+            nc.vector.tensor_copy(
+                vs_got[:].bitcast(U32).rearrange("p (r b j) -> p b r j", r=PACK, j=8),
+                vs_pool[:].bitcast(U32).indirect(offsets[:, g * LIST_COLS : (g + 1) * LIST_COLS]),
+            )
             for r in reversed(range(PACK)):
                 c = 2 * (PACK * (S_PASSES - 1 - g) + r)
-                nc.tensor.transpose(vs_cols[:, c : c + P], vs_got[:, r:PASS:PACK], ident[:])
+                nc.tensor.transpose(vs_cols[:, c : c + P], vs_got[:, r * P : (r + 1) * P], ident[:])
 
         for h, piece in enumerate(v_raw):
             nc.scalar.activation(v_pool[:, h * V_PIECE : (h + 1) * V_PIECE], piece[:], ACT.Copy)
-        v_turned = ps.tile([P, S_PASSES, 2, DV], F32, name="v_turned")
+        v_turned = ps.tile([P, S_PASSES, PACK, DV], BF16, name="v_turned")
         for g in range(S_PASSES):
             v_got = tile(f"v_got{g}", [P, PASS], BF16)
-            nc.scalar.activation(v_got[:], v_pool[:].indirect(offsets[:, g * LIST_COLS : (g + 1) * LIST_COLS]), ACT.Copy)
-            v_pairs = v_got[:].bitcast(F32)
-            for u in range(2):
-                nc.tensor.transpose(v_turned[:, g, u, :], v_pairs[:, u : PASS // 2 : 2], ident[:])
+            nc.scalar.activation(
+                v_got[:].rearrange("p (r b j) -> p b r j", r=PACK, j=8),
+                v_pool[:].indirect(offsets[:, g * LIST_COLS : (g + 1) * LIST_COLS]),
+                ACT.Copy,
+            )
+            for r in range(PACK):
+                nc.tensor.transpose(v_turned[:, g, r, :], v_got[:, r * P : (r + 1) * P], ident16[:])
         v_woven = tile("v_woven", [P, S_PASSES * DV * PACK], BF16)
         nc.scalar.copy(
-            v_woven[:].bitcast(F32).rearrange("p (g e u) -> p g e u", g=S_PASSES, u=2),
-            v_turned[:].rearrange("p g u e -> p g e u"),
+            v_woven[:].rearrange("p (g e r) -> p g e r", g=S_PASSES, r=PACK),
+            v_turned[:].rearrange("p g r e -> p g e r"),
         )
 
         th = tile("th", [P, Q_BLOCKS, DV], F32)
@@ -128,8 +136,8 @@ def tile_attend_silu_gate_topkq256n1024t2048_kernel(tc, q_words, q_scales, k_wor
             nc.vector.tensor_copy(kw_got[:], kw_pool[:].indirect(offsets[:, g * LIST_COLS : (g + 1) * LIST_COLS]))
             kw = tile(f"kw{g}", [P, D_PASSES, PASS], U16)
             nc.vector.tensor_copy(
-                kw[:].rearrange("p o (r b s) -> p o b r s", r=PACK, s=4),
-                kw_got[:].bitcast(U16).rearrange("p (b s r o) -> p o b r s", o=D_PASSES, r=PACK, s=4),
+                kw[:].rearrange("p o (r b j) -> p o b r j", r=PACK, j=8),
+                kw_got[:].bitcast(U16).rearrange("p (b r j o) -> p o b r j", o=D_PASSES, r=PACK, j=8),
             )
             for b in range(Q_BLOCKS):
                 scores = ps.tile([P, PACK, P], F32, name=f"scores{g}{b}")

from contextlib import ExitStack

import concourse.mybir as mybir
from concourse.masks import make_identity

F32 = mybir.dt.float32
BF16 = mybir.dt.bfloat16
I32 = mybir.dt.int32
U32 = mybir.dt.uint32
U16 = mybir.dt.uint16
U8 = mybir.dt.uint8
FP8X4 = mybir.dt.float8_e4m3fn_x4
FP4X4 = mybir.dt.float4_e2m1fn_x4
ACT = mybir.ActivationFunctionType
MULT = mybir.AluOpType.mult

P = 128
PACK = 4
SLOTS = 1024
POOL = 2048
D = 1024
DV = 128
NQ = 256
PASS = P * PACK
D_PASSES = D // PASS
S_PASSES = SLOTS // PASS
Q_BLOCKS = NQ // P
QUAD = 32
LIST_COLS = PASS // 16
V_PIECE = 512
KS_ROW = P - QUAD
VS_ROW = P - 1

FLOPS = 2 * NQ * SLOTS * D + 2 * NQ * SLOTS * DV


def tile_attend_silu_gate_topkq256n1024t2048_kernel(tc, q_words, q_scales, k_words, k_scales, vT, vs, og, offs, out):
    nc = tc.nc
    with ExitStack() as ctx:
        sb = ctx.enter_context(tc.tile_pool(name="sb", bufs=1))
        ps = ctx.enter_context(tc.psum_pool(name="ps", bufs=1))

        def tile(name, shape, dtype):
            return sb.tile(shape, dtype, name=name, align_bytes=64)

        offsets = sb.tile([P, SLOTS // 16], U16, name="offsets")
        ks_pool = tile("ks_pool", [P, POOL], U8)
        kw_pool = tile("kw_pool", [P, POOL], U32)
        vs_pool = tile("vs_pool", [P, POOL], F32)
        v_raw = [tile(f"v_raw{h}", [P, V_PIECE], F32) for h in range(POOL // V_PIECE)]
        v_pool = tile("v_pool", [P, POOL], BF16)
        qw = tile("qw", [P, D_PASSES, NQ], U32)
        qs = tile("qs", [P, D_PASSES, NQ], U8)
        og_sb = tile("og_sb", [P, Q_BLOCKS, DV], F32)
        ks_plane = tile("ks_plane", [P, D_PASSES * SLOTS], U8)
        zero = tile("zero", [P, 1], F32)
        zero_bias = tile("zero_bias", [P, 1], F32)
        ident = tile("ident", [P, P], F32)

        nc.vector.memset(zero[:], 0.0)
        nc.gpsimd.memset(ks_pool[:KS_ROW, :].bitcast(I32), 0)
        nc.gpsimd.memset(qs[:].rearrange("p o q -> p (o q)").bitcast(I32), 0)
        nc.gpsimd.memset(vs_pool[:VS_ROW, :], 0.0)
        nc.gpsimd.memset(ks_plane[:].bitcast(I32), 0)
        nc.scalar.activation(zero_bias[:], zero[:], ACT.Silu)
        make_identity(nc, ident[:])
        ident16 = tile("ident16", [P, P], BF16)
        make_identity(nc, ident16[:])

        nc.sync.dma_start(offsets[:], offs)
        nc.sync.dma_start(ks_pool[KS_ROW:, :].bitcast(I32), k_scales.rearrange("o f t -> (o f) t").bitcast(I32))
        nc.sync.dma_start(vs_pool[VS_ROW:, :], vs[0:1, :])
        nc.sync.dma_start(og_sb[:], og[0].rearrange("(b p) e -> p b e", p=P))
        for h, piece in enumerate(v_raw):
            nc.sync.dma_start(piece[:], vT[:, h * V_PIECE : (h + 1) * V_PIECE])
        nc.sync.dma_start(kw_pool[:].bitcast(I32), k_words[0].rearrange("p t b -> p (t b)").bitcast(I32))
        nc.sync.dma_start(qw[:].bitcast(I32), q_words[0].rearrange("o p q r -> p o (q r)").bitcast(I32))
        for quad in range(4):
            nc.sync.dma_start(
                qs[QUAD * quad : QUAD * quad + 4, :, :].bitcast(I32),
                q_scales[0, :, 4 * quad : 4 * quad + 4, :].rearrange("o f q -> f o q").bitcast(I32),
            )

        ks_got = tile("ks_got", [P, SLOTS], U8)
        nc.vector.tensor_copy(ks_got[:], ks_pool[:].indirect(offsets[:]))
        ks_dealt = tile("ks_dealt", [P, SLOTS], U8)
        nc.vector.tensor_copy(
            ks_dealt[:].bitcast(I32).rearrange("p (g r b w) -> p g b r w", g=S_PASSES, r=PACK, w=2),
            ks_got[:].bitcast(I32).rearrange("p (g b r w) -> p g b r w", g=S_PASSES, r=PACK, w=2),
        )
        for o in reversed(range(D_PASSES)):
            for quad in range(4):
                row = KS_ROW + 16 * o + 4 * quad
                nc.sync.dma_start(
                    ks_plane[QUAD * quad : QUAD * quad + 4, o * SLOTS : (o + 1) * SLOTS].bitcast(I32),
                    ks_dealt[row : row + 4, :].bitcast(I32),
                )

        vs_cols = ps.tile([P, PASS], F32, name="vs_cols")
        for g in range(S_PASSES):
            vs_got = tile(f"vs_got{g}", [P, PASS], F32)
            nc.vector.tensor_copy(
                vs_got[:].bitcast(U32).rearrange("p (r b j) -> p b r j", r=PACK, j=8),
                vs_pool[:].bitcast(U32).indirect(offsets[:, g * LIST_COLS : (g + 1) * LIST_COLS]),
            )
            for r in reversed(range(PACK)):
                c = 2 * (PACK * (S_PASSES - 1 - g) + r)
                nc.tensor.transpose(vs_cols[:, c : c + P], vs_got[:, r * P : (r + 1) * P], ident[:])

        for h, piece in enumerate(v_raw):
            nc.scalar.activation(v_pool[:, h * V_PIECE : (h + 1) * V_PIECE], piece[:], ACT.Copy)
        v_turned = ps.tile([P, S_PASSES, PACK, DV], BF16, name="v_turned")
        for g in range(S_PASSES):
            v_got = tile(f"v_got{g}", [P, PASS], BF16)
            nc.scalar.activation(
                v_got[:].rearrange("p (r b j) -> p b r j", r=PACK, j=8),
                v_pool[:].indirect(offsets[:, g * LIST_COLS : (g + 1) * LIST_COLS]),
                ACT.Copy,
            )
            for r in range(PACK):
                nc.tensor.transpose(v_turned[:, g, r, :], v_got[:, r * P : (r + 1) * P], ident16[:])
        v_woven = tile("v_woven", [P, S_PASSES * DV * PACK], BF16)
        nc.scalar.copy(
            v_woven[:].rearrange("p (g e r) -> p g e r", g=S_PASSES, r=PACK),
            v_turned[:].rearrange("p g r e -> p g e r"),
        )

        th = tile("th", [P, Q_BLOCKS, DV], F32)
        gate = tile("gate", [P, Q_BLOCKS, DV], F32)
        nc.scalar.activation(th[:], og_sb[:], ACT.Tanh, bias=zero_bias[:], scale=0.5)
        nc.scalar.activation(gate[:], th[:], ACT.Copy, bias=1.0 / 32.0, scale=1.0 / 32.0)

        p_woven = {}
        for g in range(S_PASSES):
            kw_got = tile("kw_got", [P, PASS], U32)
            nc.vector.tensor_copy(kw_got[:], kw_pool[:].indirect(offsets[:, g * LIST_COLS : (g + 1) * LIST_COLS]))
            kw = tile(f"kw{g}", [P, D_PASSES, PASS], U16)
            nc.vector.tensor_copy(
                kw[:].rearrange("p o (r b j) -> p o b r j", r=PACK, j=8),
                kw_got[:].bitcast(U16).rearrange("p (b r j o) -> p o b r j", o=D_PASSES, r=PACK, j=8),
            )
            for b in range(Q_BLOCKS):
                scores = ps.tile([P, PACK, P], F32, name=f"scores{g}{b}")
                for r in range(PACK):
                    for o in range(D_PASSES):
                        nc.tensor.matmul_mx(
                            out=scores[:, r, :],
                            lhsT=kw[:, o, r * P : (r + 1) * P].bitcast(FP4X4),
                            lhsT_scale=ks_plane[:, o * SLOTS + g * PASS + r * P : o * SLOTS + g * PASS + (r + 1) * P],
                            rhs=qw[:, o, b * P : (b + 1) * P].bitcast(FP8X4),
                            rhs_scale=qs[:, o, b * P : (b + 1) * P],
                            start=(o == 0),
                            stop=(o == D_PASSES - 1),
                        )
                p_woven[g, b] = tile(f"p{g}{b}", [P, P, PACK], F32)
                nc.scalar.activation(p_woven[g, b][:], scores[:].rearrange("p r q -> p q r"), ACT.Silu, bias=zero_bias[:])

        v_codes = tile("v_codes", [P, S_PASSES * DV], U32)
        v_scales = tile("v_scales", [P, S_PASSES * DV], U8)
        nc.vector.quantize_mx(out=v_codes[:].bitcast(FP8X4), scales=v_scales[:], in_=v_woven[:])

        w_codes, w_scales = {}, {}
        for g in range(S_PASSES):
            first = 2 * PACK * (S_PASSES - 1 - g) + VS_ROW
            vs_by_place = vs_cols[:, first : first + 2 * PACK : 2].unsqueeze(1).to_broadcast([P, P, PACK])
            for b in range(Q_BLOCKS):
                w = tile(f"w{g}{b}", [P, P, PACK], BF16)
                nc.vector.tensor_tensor(w[:], p_woven[g, b][:], vs_by_place, MULT)
                w_codes[g, b] = tile(f"w_codes{g}{b}", [P, P], U32)
                w_scales[g, b] = tile(f"w_scales{g}{b}", [P, P], U8)
                nc.vector.quantize_mx(
                    out=w_codes[g, b][:].bitcast(FP8X4),
                    scales=w_scales[g, b][:],
                    in_=w[:].rearrange("p q r -> p (q r)"),
                )

        for b in range(Q_BLOCKS):
            y = ps.tile([P, DV], F32, name=f"y{b}")
            for g in range(S_PASSES):
                nc.tensor.matmul_mx(
                    out=y[:],
                    lhsT=w_codes[g, b][:].bitcast(FP8X4),
                    lhsT_scale=w_scales[g, b][:],
                    rhs=v_codes[:, g * DV : (g + 1) * DV].bitcast(FP8X4),
                    rhs_scale=v_scales[:, g * DV : (g + 1) * DV],
                    start=(g == 0),
                    stop=(g == S_PASSES - 1),
                )
            res = tile(f"res{b}", [P, DV], F32)
            nc.vector.tensor_tensor(res[:], y[:], gate[:, b, :], MULT)
            nc.sync.dma_start(out[0, b * P : (b + 1) * P, :], res[:])
